import numpy as np, ml_dtypes
CORES = [71,199,95,223,103,231,111,239,119,247,127,255]
N = 12
KB, QP = 1, 128
MEM = [1,4,6,10]
def setup_inputs(rng):
    return {"q": rng.standard_normal((N, 128, QP), dtype=np.float32).astype(ml_dtypes.bfloat16), "k": rng.standard_normal((N, 128, KB * 128), dtype=np.float32).astype(ml_dtypes.bfloat16), "v": rng.standard_normal((N, 128, KB * 128), dtype=np.float32).astype(ml_dtypes.bfloat16)}
def setup_inputs_big(rng):
    d = setup_inputs(rng)
    for k in ("q", "k", "v"): d[k] = (d[k].astype(np.float32) * 1024.0).astype(d[k].dtype)
    return d
def setup_inputs_small(rng):
    d = setup_inputs(rng)
    for k in ("q", "k", "v"): d[k] = (d[k].astype(np.float32) * (1 / 1024.0)).astype(d[k].dtype)
    return d
def setup_inputs_apart(rng):
    d = setup_inputs(rng)
    f = (10.0 ** rng.permutation(np.linspace(-1.5, 1.5, N))).astype(np.float32).reshape(N, 1, 1)
    for k in ("q", "k", "v"): d[k] = (d[k].astype(np.float32) * f).astype(d[k].dtype)
    return d
def reference(q, k, v):
    Q, K, V = q.astype(np.float64), k.astype(np.float64), v.astype(np.float64)
    y = np.zeros((N, 128, QP))
    for r in range(N):
        for j in MEM:
            for b in range(KB):
                S = np.maximum(K[j][:, 128 * b:128 * b + 128].T @ Q[r], 0.0)
                y[r] += V[j][:, 128 * b:128 * b + 128].T @ S
    return {"y": y.astype(ml_dtypes.bfloat16 if q.dtype != np.float64 else np.float64)}

@@ -1,0 +1,161 @@
+from concourse.bass import DstId, RemoteDMATransfer
+from concourse.mybir import AluOpType
+
+P = 128
+NM = 4
+CL = 2
+RC = CL * P
+
+SCRATCH = {
+    "kv": ("sbuf", [P, NM * 2 * P], "bfloat16"),
+    "qq": ("sbuf", [P, RC + P], "bfloat16"),
+    "zero": ("sbuf", [P, NM * P], "float32"),
+    "sr": ("sbuf", [P, NM * RC], "bfloat16"),
+    "sl": ("sbuf", [P, NM * P], "bfloat16"),
+    "yo": ("sbuf", [P, RC + P], "bfloat16"),
+    "yl": ("dram", [P, P], "bfloat16"),
+    "pr0": ("psum", [P, 512], "float32"),
+    "pr1": ("psum", [P, 512], "float32"),
+    "pr2": ("psum", [P, 512], "float32"),
+    "pr3": ("psum", [P, 512], "float32"),
+    "pl": ("psum", [P, 512], "float32"),
+    "por": ("psum", [P, 512], "float32"),
+    "pol": ("psum", [P, 512], "float32"),
+}
+SEMAPHORES = (["ldkv", "ldq", "zs", "qin", "yin", "sent", "st", "m2r", "cr", "al", "rl", "m2l", "cl"]
+              + ["kv%d" % i for i in range(NM)] + ["a%d" % i for i in range(NM)] + ["r%d" % i for i in range(NM)])
+
+
+def _engines(mask):
+    return [1 << b for b in range(mask.bit_length()) if (mask >> b) & 1]
+
+
+def _join(bits):
+    m = 0
+    for b in bits:
+        m |= b
+    return m
+
+
+def _plan(T, topo):
+    sites = [T.cores[j] for j in T.tables["MEM"]]
+    served = {s: [] for s in sites}
+    for c in T.cores:
+        if c in served:
+            continue
+        free = [s for s in sites if len(served[s]) < CL and topo.may_write(c, s) and topo.may_write(s, c)]
+        best = min(free, key=lambda s: (not topo.same_plane(c, s), len(served[s]), sites.index(s)))
+        served[best].append(c)
+    return sites, served
+
+
+def _dst(topo, dst, src):
+    rid, pid = topo.addr(dst, src)
+    return DstId(rid=rid, pnc=pid)
+
+
+def _client(g, core, T, topo, site, slot):
+    own = T.qq[:, RC:RC + P]
+    g.sync.dma_start(own, T.q[:, :]).then_inc(T.sem.ldq, 16)
+    mask = topo.mask(core, site)
+    n = len(_engines(mask))
+    rid, pid = topo.addr(site, core)
+    g.wait_ge(T.sem.ldq, 16)
+    g.remote_dma(T.qq[:, slot * P:(slot + 1) * P], own, T.sem.qin, T.sem.sent, pid, rid, mask)
+    back = len(_engines(topo.mask(site, core))) // CL
+    g.sync.wait_ge(T.sem.yin, back)
+    g.sync.dma_start(T.y[:, :], T.yl[:, :]).then_inc(T.sem.st, 16)
+    g.sync.wait_ge(T.sem.st, 16)
+    g.wait_ge(T.sem.sent, n)
+
+
+def _site(g, core, T, topo, sites, clients):
+    m = sites.index(core)
+    others = [(m + d) % NM for d in range(1, NM)]
+
+    def kslot(i):
+        return T.kv[:, i * 2 * P:i * 2 * P + P]
+
+    def vslot(i):
+        return T.kv[:, i * 2 * P + P:(i + 1) * 2 * P]
+
+    pr = [T.pr0, T.pr1, T.pr2, T.pr3]
+    g.sync.dma_start(kslot(m), T.k[:, :]).then_inc(T.sem.ldkv, 16)
+    g.scalar.dma_start(vslot(m), T.v[:, :]).then_inc(T.sem.ldkv, 16)
+    g.sync.dma_start(T.qq[:, RC:RC + P], T.q[:, :]).then_inc(T.sem.ldq, 16)
+    g.vector.memset(T.zero[:, :], 0.0).then_inc(T.sem.zs, 1)
+
+    slot = T.kv[:, m * 2 * P:(m + 1) * 2 * P]
+    kvmask = topo.mask(core, sites[others[0]])
+    for i in others:
+        kvmask &= topo.mask(core, sites[i])
+    nkv = len(_engines(kvmask))
+    g.wait_ge(T.sem.ldkv, 32)
+    g.remote_dma_fused([RemoteDMATransfer(dst_ids=[_dst(topo, sites[i], core) for i in others], dma_engine_mask=kvmask,
+                                          remote_sem=T.sem["kv%d" % m], srcs=[slot], dsts=[slot for _ in others])],
+                       local_sem=T.sem.sent)
+
+    te = g.tensor
+    nq = sum(len(_engines(topo.mask(c, core))) for c in clients)
+    te.wait_ge(T.sem.ldkv, 32)
+    te.wait_ge(T.sem.qin, nq)
+    te.matmul(pr[m][:, 0:RC], kslot(m), T.qq[:, 0:RC], start=True, stop=True).then_inc(T.sem["a%d" % m], 1)
+    te.wait_ge(T.sem.ldq, 16)
+    te.matmul(T.pl[:, m * P:(m + 1) * P], kslot(m), T.qq[:, RC:RC + P], start=True, stop=True).then_inc(T.sem.al, 1)
+    te.wait_ge(T.sem["r%d" % m], 1)
+    te.matmul(T.por[:, 0:RC], vslot(m), T.sr[:, m * RC:(m + 1) * RC], start=True, stop=False)
+    for i in others:
+        te.wait_ge(T.sem["kv%d" % i], len(_engines(topo.mask(sites[i], core))))
+        te.matmul(pr[i][:, 0:RC], kslot(i), T.qq[:, 0:RC], start=True, stop=True).then_inc(T.sem["a%d" % i], 1)
+    for i in others:
+        te.wait_ge(T.sem["r%d" % i], 1)
+        last = i == others[-1]
+        mm = te.matmul(T.por[:, 0:RC], vslot(i), T.sr[:, i * RC:(i + 1) * RC], start=False, stop=last)
+        if last:
+            mm.then_inc(T.sem.m2r, 1)
+    for i in others:
+        te.matmul(T.pl[:, i * P:(i + 1) * P], kslot(i), T.qq[:, RC:RC + P], start=True, stop=True).then_inc(T.sem.al, 1)
+    te.wait_ge(T.sem.rl, 1)
+    for i in range(NM):
+        mm = te.matmul(T.pol[:, 0:P], vslot(i), T.sl[:, i * P:(i + 1) * P], start=(i == 0), stop=(i == NM - 1))
+        if i == NM - 1:
+            mm.then_inc(T.sem.m2l, 1)
+
+    ve = g.vector
+    ve.wait_ge(T.sem.zs, 1)
+    for i in [m] + others:
+        ve.wait_ge(T.sem["a%d" % i], 1)
+        ve.tensor_tensor(T.sr[:, i * RC:(i + 1) * RC], pr[i][:, 0:RC], T.zero[:, 0:RC], AluOpType.max).then_inc(T.sem["r%d" % i], 1)
+    ve.wait_ge(T.sem.m2r, 1)
+    ve.tensor_copy(T.yo[:, 0:RC], T.por[:, 0:RC]).then_inc(T.sem.cr, 1)
+    ve.wait_ge(T.sem.al, NM)
+    ve.tensor_tensor(T.sl[:, :], T.pl[:, 0:NM * P], T.zero[:, :], AluOpType.max).then_inc(T.sem.rl, 1)
+    ve.wait_ge(T.sem.m2l, 1)
+    ve.tensor_copy(T.yo[:, RC:RC + P], T.pol[:, 0:P]).then_inc(T.sem.cl, 1)
+
+    ymask = topo.mask(core, clients[0])
+    for c in clients:
+        ymask &= topo.mask(core, c)
+    eng = _engines(ymask)
+    share = len(eng) // CL
+    g.wait_ge(T.sem.cr, 1)
+    g.remote_dma_fused([RemoteDMATransfer(dst_ids=[_dst(topo, c, core)], dma_engine_mask=_join(eng[s * share:(s + 1) * share]),
+                                          remote_sem=T.sem.yin, src=T.yo[:, s * P:(s + 1) * P], dst=T.yl[:, :])
+                        for s, c in enumerate(clients)], local_sem=T.sem.sent)
+
+    g.sync.wait_ge(T.sem.cl, 1)
+    g.sync.dma_start(T.y[:, :], T.yo[:, RC:RC + P]).then_inc(T.sem.st, 16)
+    g.sync.wait_ge(T.sem.st, 16)
+    g.wait_ge(T.sem.sent, nkv + share * CL)
+
+
+def rank_program(g, core, T, topo):
+    if T.rank_of(core) is None:
+        return
+    sites, served = _plan(T, topo)
+    if core in served:
+        _site(g, core, T, topo, sites, served[core])
+        return
+    for s in sites:
+        if core in served[s]:
+            _client(g, core, T, topo, s, served[s].index(core))

@@ -9,20 +9,23 @@ RC = CL * P
 SCRATCH = {
     "kv": ("sbuf", [P, NM * 2 * P], "bfloat16"),
     "qq": ("sbuf", [P, RC + P], "bfloat16"),
-    "zero": ("sbuf", [P, NM * P], "float32"),
+    "qd": ("dram", [P, P], "bfloat16"),
+    "zero": ("sbuf", [P, 3 * P], "float32"),
     "sr": ("sbuf", [P, NM * RC], "bfloat16"),
     "sl": ("sbuf", [P, NM * P], "bfloat16"),
     "yo": ("sbuf", [P, RC + P], "bfloat16"),
     "yl": ("dram", [P, P], "bfloat16"),
-    "pr0": ("psum", [P, 512], "float32"),
-    "pr1": ("psum", [P, 512], "float32"),
-    "pr2": ("psum", [P, 512], "float32"),
-    "pr3": ("psum", [P, 512], "float32"),
+    "px": ("psum", [P, 512], "float32"),
+    "py": ("psum", [P, 512], "float32"),
+    "pa": ("psum", [P, 512], "float32"),
+    "pb": ("psum", [P, 512], "float32"),
     "pl": ("psum", [P, 512], "float32"),
-    "por": ("psum", [P, 512], "float32"),
+    "poa": ("psum", [P, 512], "float32"),
+    "pob": ("psum", [P, 512], "float32"),
     "pol": ("psum", [P, 512], "float32"),
 }
-SEMAPHORES = (["ldkv", "ldq", "zs", "qin", "yin", "sent", "st", "m2r", "cr", "al", "rl", "m2l", "cl"]
+SEMAPHORES = (["ldkv", "ldq", "zs", "qin", "yin", "sent", "st", "ab", "rb", "m2a", "m2b", "cr",
+               "al1", "al3", "rl1", "rl3", "m2l", "cl"]
               + ["kv%d" % i for i in range(NM)] + ["a%d" % i for i in range(NM)] + ["r%d" % i for i in range(NM)])
 
 
@@ -49,19 +52,34 @@ def _plan(T, topo):
     return sites, served
 
 
+def _rounds(sites, topo):
+    def far(a, b):
+        if topo.mates(sites[a], sites[b]):
+            return 0
+        return 1 if topo.same_plane(sites[a], sites[b]) else 2
+
+    rounds = []
+    for x in range(1, NM):
+        y, z = [i for i in range(1, NM) if i != x]
+        partner = [0] * NM
+        partner[0], partner[x], partner[y], partner[z] = x, 0, z, y
+        rounds.append(((max(far(0, x), far(y, z)), far(0, x) + far(y, z)), partner))
+    rounds.sort(key=lambda r: r[0])
+    return [r[1] for r in rounds]
+
+
 def _dst(topo, dst, src):
     rid, pid = topo.addr(dst, src)
     return DstId(rid=rid, pnc=pid)
 
 
 def _client(g, core, T, topo, site, slot):
-    own = T.qq[:, RC:RC + P]
-    g.sync.dma_start(own, T.q[:, :]).then_inc(T.sem.ldq, 16)
+    g.sync.dma_start(T.qd[:, :], T.q[:, :]).then_inc(T.sem.ldq, 16)
     mask = topo.mask(core, site)
     n = len(_engines(mask))
     rid, pid = topo.addr(site, core)
     g.wait_ge(T.sem.ldq, 16)
-    g.remote_dma(T.qq[:, slot * P:(slot + 1) * P], own, T.sem.qin, T.sem.sent, pid, rid, mask)
+    g.remote_dma(T.qq[:, slot * P:(slot + 1) * P], T.qd[:, :], T.sem.qin, T.sem.sent, pid, rid, mask)
     back = len(_engines(topo.mask(site, core))) // CL
     g.sync.wait_ge(T.sem.yin, back)
     g.sync.dma_start(T.y[:, :], T.yl[:, :]).then_inc(T.sem.st, 16)
@@ -71,82 +89,119 @@ def _client(g, core, T, topo, site, slot):
 
 def _site(g, core, T, topo, sites, clients):
     m = sites.index(core)
-    others = [(m + d) % NM for d in range(1, NM)]
+    send_to = [partner[m] for partner in _rounds(sites, topo)]
+    src = [m] + send_to
 
-    def kslot(i):
-        return T.kv[:, i * 2 * P:i * 2 * P + P]
+    def kk(t):
+        return T.kv[:, src[t] * 2 * P:src[t] * 2 * P + P]
 
-    def vslot(i):
-        return T.kv[:, i * 2 * P + P:(i + 1) * 2 * P]
+    def vv(t):
+        return T.kv[:, src[t] * 2 * P + P:(src[t] + 1) * 2 * P]
 
-    pr = [T.pr0, T.pr1, T.pr2, T.pr3]
-    g.sync.dma_start(kslot(m), T.k[:, :]).then_inc(T.sem.ldkv, 16)
-    g.scalar.dma_start(vslot(m), T.v[:, :]).then_inc(T.sem.ldkv, 16)
-    g.sync.dma_start(T.qq[:, RC:RC + P], T.q[:, :]).then_inc(T.sem.ldq, 16)
-    g.vector.memset(T.zero[:, :], 0.0).then_inc(T.sem.zs, 1)
+    def sa(t):
+        return T.sr[:, t * RC:t * RC + P]
+
+    def sb(t):
+        return T.sr[:, t * RC + P:(t + 1) * RC]
+
+    def sl(t):
+        return T.sl[:, t * P:(t + 1) * P]
+
+    qr, qa, qb, ql = T.qq[:, 0:RC], T.qq[:, 0:P], T.qq[:, P:RC], T.qq[:, RC:RC + P]
+    sem = T.sem
+    g.sync.dma_start(kk(0), T.k[:, :]).then_inc(sem.ldkv, 16)
+    g.scalar.dma_start(vv(0), T.v[:, :]).then_inc(sem.ldkv, 16)
+    g.sync.wait_ge(sem.ldkv, 32)
+    g.sync.dma_start(ql, T.q[:, :]).then_inc(sem.ldq, 16)
+    g.vector.memset(T.zero[:, :], 0.0).then_inc(sem.zs, 1)
 
     slot = T.kv[:, m * 2 * P:(m + 1) * 2 * P]
-    kvmask = topo.mask(core, sites[others[0]])
-    for i in others:
+    kvmask = topo.mask(core, sites[send_to[0]])
+    for i in send_to:
         kvmask &= topo.mask(core, sites[i])
     nkv = len(_engines(kvmask))
-    g.wait_ge(T.sem.ldkv, 32)
-    g.remote_dma_fused([RemoteDMATransfer(dst_ids=[_dst(topo, sites[i], core) for i in others], dma_engine_mask=kvmask,
-                                          remote_sem=T.sem["kv%d" % m], srcs=[slot], dsts=[slot for _ in others])],
-                       local_sem=T.sem.sent)
+    g.wait_ge(sem.ldkv, 32)
+    g.remote_dma_fused([RemoteDMATransfer(dst_ids=[_dst(topo, sites[i], core) for i in send_to], dma_engine_mask=kvmask,
+                                          remote_sem=sem["kv%d" % m], srcs=[slot], dsts=[slot for _ in send_to])],
+                       local_sem=sem.sent)
 
     te = g.tensor
     nq = sum(len(_engines(topo.mask(c, core))) for c in clients)
-    te.wait_ge(T.sem.ldkv, 32)
-    te.wait_ge(T.sem.qin, nq)
-    te.matmul(pr[m][:, 0:RC], kslot(m), T.qq[:, 0:RC], start=True, stop=True).then_inc(T.sem["a%d" % m], 1)
-    te.wait_ge(T.sem.ldq, 16)
-    te.matmul(T.pl[:, m * P:(m + 1) * P], kslot(m), T.qq[:, RC:RC + P], start=True, stop=True).then_inc(T.sem.al, 1)
-    te.wait_ge(T.sem["r%d" % m], 1)
-    te.matmul(T.por[:, 0:RC], vslot(m), T.sr[:, m * RC:(m + 1) * RC], start=True, stop=False)
-    for i in others:
-        te.wait_ge(T.sem["kv%d" % i], len(_engines(topo.mask(sites[i], core))))
-        te.matmul(pr[i][:, 0:RC], kslot(i), T.qq[:, 0:RC], start=True, stop=True).then_inc(T.sem["a%d" % i], 1)
-    for i in others:
-        te.wait_ge(T.sem["r%d" % i], 1)
-        last = i == others[-1]
-        mm = te.matmul(T.por[:, 0:RC], vslot(i), T.sr[:, i * RC:(i + 1) * RC], start=False, stop=last)
-        if last:
-            mm.then_inc(T.sem.m2r, 1)
-    for i in others:
-        te.matmul(T.pl[:, i * P:(i + 1) * P], kslot(i), T.qq[:, RC:RC + P], start=True, stop=True).then_inc(T.sem.al, 1)
-    te.wait_ge(T.sem.rl, 1)
-    for i in range(NM):
-        mm = te.matmul(T.pol[:, 0:P], vslot(i), T.sl[:, i * P:(i + 1) * P], start=(i == 0), stop=(i == NM - 1))
-        if i == NM - 1:
-            mm.then_inc(T.sem.m2l, 1)
+
+    def arrived(t):
+        te.wait_ge(sem["kv%d" % src[t]], len(_engines(topo.mask(sites[src[t]], core))))
+
+    te.wait_ge(sem.ldkv, 32)
+    te.wait_ge(sem.qin, nq)
+    te.matmul(T.px[:, 0:RC], kk(0), qr, start=True, stop=True).then_inc(sem.a0, 1)
+    arrived(1)
+    te.matmul(T.py[:, 0:RC], kk(1), qr, start=True, stop=True).then_inc(sem.a1, 1)
+    te.wait_ge(sem.r0, 1)
+    te.matmul(T.poa[:, 0:P], vv(0), sa(0), start=True, stop=False)
+    te.matmul(T.pob[:, 0:P], vv(0), sb(0), start=True, stop=False)
+    arrived(2)
+    te.matmul(T.px[:, 0:RC], kk(2), qr, start=True, stop=True).then_inc(sem.a2, 1)
+    te.wait_ge(sem.r1, 1)
+    te.matmul(T.poa[:, 0:P], vv(1), sa(1), start=False, stop=False)
+    te.matmul(T.pob[:, 0:P], vv(1), sb(1), start=False, stop=False)
+    arrived(3)
+    te.matmul(T.pa[:, 0:P], kk(3), qa, start=True, stop=True).then_inc(sem.a3, 1)
+    te.matmul(T.pb[:, 0:P], kk(3), qb, start=True, stop=True).then_inc(sem.ab, 1)
+    te.wait_ge(sem.r2, 1)
+    te.matmul(T.poa[:, 0:P], vv(2), sa(2), start=False, stop=False)
+    te.matmul(T.pob[:, 0:P], vv(2), sb(2), start=False, stop=False)
+    te.wait_ge(sem.r3, 1)
+    te.matmul(T.poa[:, 0:P], vv(3), sa(3), start=False, stop=True).then_inc(sem.m2a, 1)
+    te.wait_ge(sem.rb, 1)
+    te.matmul(T.pob[:, 0:P], vv(3), sb(3), start=False, stop=True).then_inc(sem.m2b, 1)
+    te.wait_ge(sem.ldq, 16)
+    for t in range(NM - 1):
+        te.matmul(T.pl[:, t * P:(t + 1) * P], kk(t), ql, start=True, stop=True).then_inc(sem.al1, 1)
+    te.matmul(T.py[:, 0:P], kk(3), ql, start=True, stop=True).then_inc(sem.al3, 1)
+    te.wait_ge(sem.rl1, 1)
+    for t in range(NM - 1):
+        te.matmul(T.pol[:, 0:P], vv(t), sl(t), start=(t == 0), stop=False)
+    te.wait_ge(sem.rl3, 1)
+    te.matmul(T.pol[:, 0:P], vv(3), sl(3), start=False, stop=True).then_inc(sem.m2l, 1)
 
     ve = g.vector
-    ve.wait_ge(T.sem.zs, 1)
-    for i in [m] + others:
-        ve.wait_ge(T.sem["a%d" % i], 1)
-        ve.tensor_tensor(T.sr[:, i * RC:(i + 1) * RC], pr[i][:, 0:RC], T.zero[:, 0:RC], AluOpType.max).then_inc(T.sem["r%d" % i], 1)
-    ve.wait_ge(T.sem.m2r, 1)
-    ve.tensor_copy(T.yo[:, 0:RC], T.por[:, 0:RC]).then_inc(T.sem.cr, 1)
-    ve.wait_ge(T.sem.al, NM)
-    ve.tensor_tensor(T.sl[:, :], T.pl[:, 0:NM * P], T.zero[:, :], AluOpType.max).then_inc(T.sem.rl, 1)
-    ve.wait_ge(T.sem.m2l, 1)
-    ve.tensor_copy(T.yo[:, RC:RC + P], T.pol[:, 0:P]).then_inc(T.sem.cl, 1)
+    mx = AluOpType.max
+    ve.wait_ge(sem.zs, 1)
+    ve.wait_ge(sem.a0, 1)
+    ve.tensor_tensor(T.sr[:, 0:RC], T.px[:, 0:RC], T.zero[:, 0:RC], mx).then_inc(sem.r0, 1)
+    ve.wait_ge(sem.a1, 1)
+    ve.tensor_tensor(T.sr[:, RC:2 * RC], T.py[:, 0:RC], T.zero[:, 0:RC], mx).then_inc(sem.r1, 1)
+    ve.wait_ge(sem.a2, 1)
+    ve.tensor_tensor(T.sr[:, 2 * RC:3 * RC], T.px[:, 0:RC], T.zero[:, 0:RC], mx).then_inc(sem.r2, 1)
+    ve.wait_ge(sem.a3, 1)
+    ve.tensor_tensor(sa(3), T.pa[:, 0:P], T.zero[:, 0:P], mx).then_inc(sem.r3, 1)
+    ve.wait_ge(sem.ab, 1)
+    ve.tensor_tensor(sb(3), T.pb[:, 0:P], T.zero[:, 0:P], mx).then_inc(sem.rb, 1)
+    ve.wait_ge(sem.m2a, 1)
+    ve.tensor_copy(T.yo[:, 0:P], T.poa[:, 0:P]).then_inc(sem.cr, 1)
+    ve.wait_ge(sem.m2b, 1)
+    ve.tensor_copy(T.yo[:, P:RC], T.pob[:, 0:P]).then_inc(sem.cr, 1)
+    ve.wait_ge(sem.al1, NM - 1)
+    ve.tensor_tensor(T.sl[:, 0:3 * P], T.pl[:, 0:3 * P], T.zero[:, 0:3 * P], mx).then_inc(sem.rl1, 1)
+    ve.wait_ge(sem.al3, 1)
+    ve.tensor_tensor(sl(3), T.py[:, 0:P], T.zero[:, 0:P], mx).then_inc(sem.rl3, 1)
+    ve.wait_ge(sem.m2l, 1)
+    ve.tensor_copy(T.yo[:, RC:RC + P], T.pol[:, 0:P]).then_inc(sem.cl, 1)
 
     ymask = topo.mask(core, clients[0])
     for c in clients:
         ymask &= topo.mask(core, c)
     eng = _engines(ymask)
     share = len(eng) // CL
-    g.wait_ge(T.sem.cr, 1)
+    g.wait_ge(sem.cr, CL)
     g.remote_dma_fused([RemoteDMATransfer(dst_ids=[_dst(topo, c, core)], dma_engine_mask=_join(eng[s * share:(s + 1) * share]),
-                                          remote_sem=T.sem.yin, src=T.yo[:, s * P:(s + 1) * P], dst=T.yl[:, :])
-                        for s, c in enumerate(clients)], local_sem=T.sem.sent)
+                                          remote_sem=sem.yin, src=T.yo[:, s * P:(s + 1) * P], dst=T.yl[:, :])
+                        for s, c in enumerate(clients)], local_sem=sem.sent)
 
-    g.sync.wait_ge(T.sem.cl, 1)
-    g.sync.dma_start(T.y[:, :], T.yo[:, RC:RC + P]).then_inc(T.sem.st, 16)
-    g.sync.wait_ge(T.sem.st, 16)
-    g.wait_ge(T.sem.sent, nkv + share * CL)
+    g.sync.wait_ge(sem.cl, 1)
+    g.sync.dma_start(T.y[:, :], T.yo[:, RC:RC + P]).then_inc(sem.st, 16)
+    g.sync.wait_ge(sem.st, 16)
+    g.wait_ge(sem.sent, nkv + share * CL)
 
 
 def rank_program(g, core, T, topo):

from concourse.bass import DstId, RemoteDMATransfer
from concourse.mybir import AluOpType

P = 128
NM = 4
CL = 2
RC = CL * P

SCRATCH = {
    "kv": ("sbuf", [P, NM * 2 * P], "bfloat16"),
    "qq": ("sbuf", [P, RC + P], "bfloat16"),
    "qd": ("dram", [P, P], "bfloat16"),
    "zero": ("sbuf", [P, 3 * P], "float32"),
    "sr": ("sbuf", [P, NM * RC], "bfloat16"),
    "sl": ("sbuf", [P, NM * P], "bfloat16"),
    "yo": ("sbuf", [P, RC + P], "bfloat16"),
    "yl": ("dram", [P, P], "bfloat16"),
    "px": ("psum", [P, 512], "float32"),
    "py": ("psum", [P, 512], "float32"),
    "pa": ("psum", [P, 512], "float32"),
    "pb": ("psum", [P, 512], "float32"),
    "pl": ("psum", [P, 512], "float32"),
    "poa": ("psum", [P, 512], "float32"),
    "pob": ("psum", [P, 512], "float32"),
    "pol": ("psum", [P, 512], "float32"),
}
SEMAPHORES = (["ldkv", "ldq", "zs", "qin", "yin", "sent", "st", "ab", "rb", "m2a", "m2b", "cr",
               "al1", "al3", "rl1", "rl3", "m2l", "cl"]
              + ["kv%d" % i for i in range(NM)] + ["a%d" % i for i in range(NM)] + ["r%d" % i for i in range(NM)])


def _engines(mask):
    return [1 << b for b in range(mask.bit_length()) if (mask >> b) & 1]


def _join(bits):
    m = 0
    for b in bits:
        m |= b
    return m


def _plan(T, topo):
    sites = [T.cores[j] for j in T.tables["MEM"]]
    served = {s: [] for s in sites}
    for c in T.cores:
        if c in served:
            continue
        free = [s for s in sites if len(served[s]) < CL and topo.may_write(c, s) and topo.may_write(s, c)]
        best = min(free, key=lambda s: (not topo.same_plane(c, s), len(served[s]), sites.index(s)))
        served[best].append(c)
    return sites, served


def _rounds(sites, topo):
    def far(a, b):
        if topo.mates(sites[a], sites[b]):
            return 0
        return 1 if topo.same_plane(sites[a], sites[b]) else 2

    rounds = []
    for x in range(1, NM):
        y, z = [i for i in range(1, NM) if i != x]
        partner = [0] * NM
        partner[0], partner[x], partner[y], partner[z] = x, 0, z, y
        rounds.append(((max(far(0, x), far(y, z)), far(0, x) + far(y, z)), partner))
    rounds.sort(key=lambda r: r[0])
    return [r[1] for r in rounds]


def _dst(topo, dst, src):
    rid, pid = topo.addr(dst, src)
    return DstId(rid=rid, pnc=pid)


def _client(g, core, T, topo, site, slot):
    g.sync.dma_start(T.qd[:, :], T.q[:, :]).then_inc(T.sem.ldq, 16)
    mask = topo.mask(core, site)
    n = len(_engines(mask))
    rid, pid = topo.addr(site, core)
    g.wait_ge(T.sem.ldq, 16)
    g.remote_dma(T.qq[:, slot * P:(slot + 1) * P], T.qd[:, :], T.sem.qin, T.sem.sent, pid, rid, mask)
    back = len(_engines(topo.mask(site, core))) // CL
    g.sync.wait_ge(T.sem.yin, back)
    g.sync.dma_start(T.y[:, :], T.yl[:, :]).then_inc(T.sem.st, 16)
    g.sync.wait_ge(T.sem.st, 16)
    g.wait_ge(T.sem.sent, n)


def _site(g, core, T, topo, sites, clients):
    m = sites.index(core)
    send_to = [partner[m] for partner in _rounds(sites, topo)]
    src = [m] + send_to

    def kk(t):
        return T.kv[:, src[t] * 2 * P:src[t] * 2 * P + P]

    def vv(t):
        return T.kv[:, src[t] * 2 * P + P:(src[t] + 1) * 2 * P]

    def sa(t):
        return T.sr[:, t * RC:t * RC + P]

    def sb(t):
        return T.sr[:, t * RC + P:(t + 1) * RC]

    def sl(t):
        return T.sl[:, t * P:(t + 1) * P]

    qr, qa, qb, ql = T.qq[:, 0:RC], T.qq[:, 0:P], T.qq[:, P:RC], T.qq[:, RC:RC + P]
    sem = T.sem
    g.sync.dma_start(kk(0), T.k[:, :]).then_inc(sem.ldkv, 16)
    g.scalar.dma_start(vv(0), T.v[:, :]).then_inc(sem.ldkv, 16)
    g.sync.wait_ge(sem.ldkv, 32)
    g.sync.dma_start(ql, T.q[:, :]).then_inc(sem.ldq, 16)
    g.vector.memset(T.zero[:, :], 0.0).then_inc(sem.zs, 1)

    slot = T.kv[:, m * 2 * P:(m + 1) * 2 * P]
    kvmask = topo.mask(core, sites[send_to[0]])
    for i in send_to:
        kvmask &= topo.mask(core, sites[i])
    nkv = len(_engines(kvmask))
    g.wait_ge(sem.ldkv, 32)
    g.remote_dma_fused([RemoteDMATransfer(dst_ids=[_dst(topo, sites[i], core) for i in send_to], dma_engine_mask=kvmask,
                                          remote_sem=sem["kv%d" % m], srcs=[slot], dsts=[slot for _ in send_to])],
                       local_sem=sem.sent)

    te = g.tensor
    nq = sum(len(_engines(topo.mask(c, core))) for c in clients)

    def arrived(t):
        te.wait_ge(sem["kv%d" % src[t]], len(_engines(topo.mask(sites[src[t]], core))))

    te.wait_ge(sem.ldkv, 32)
    te.wait_ge(sem.qin, nq)
    te.matmul(T.px[:, 0:RC], kk(0), qr, start=True, stop=True).then_inc(sem.a0, 1)
    arrived(1)
    te.matmul(T.py[:, 0:RC], kk(1), qr, start=True, stop=True).then_inc(sem.a1, 1)
    te.wait_ge(sem.r0, 1)
    te.matmul(T.poa[:, 0:P], vv(0), sa(0), start=True, stop=False)
    te.matmul(T.pob[:, 0:P], vv(0), sb(0), start=True, stop=False)
    arrived(2)
    te.matmul(T.px[:, 0:RC], kk(2), qr, start=True, stop=True).then_inc(sem.a2, 1)
    te.wait_ge(sem.r1, 1)
    te.matmul(T.poa[:, 0:P], vv(1), sa(1), start=False, stop=False)
    te.matmul(T.pob[:, 0:P], vv(1), sb(1), start=False, stop=False)
    arrived(3)
    te.matmul(T.pa[:, 0:P], kk(3), qa, start=True, stop=True).then_inc(sem.a3, 1)
    te.matmul(T.pb[:, 0:P], kk(3), qb, start=True, stop=True).then_inc(sem.ab, 1)
    te.wait_ge(sem.r2, 1)
    te.matmul(T.poa[:, 0:P], vv(2), sa(2), start=False, stop=False)
    te.matmul(T.pob[:, 0:P], vv(2), sb(2), start=False, stop=False)
    te.wait_ge(sem.r3, 1)
    te.matmul(T.poa[:, 0:P], vv(3), sa(3), start=False, stop=True).then_inc(sem.m2a, 1)
    te.wait_ge(sem.rb, 1)
    te.matmul(T.pob[:, 0:P], vv(3), sb(3), start=False, stop=True).then_inc(sem.m2b, 1)
    te.wait_ge(sem.ldq, 16)
    for t in range(NM - 1):
        te.matmul(T.pl[:, t * P:(t + 1) * P], kk(t), ql, start=True, stop=True).then_inc(sem.al1, 1)
    te.matmul(T.py[:, 0:P], kk(3), ql, start=True, stop=True).then_inc(sem.al3, 1)
    te.wait_ge(sem.rl1, 1)
    for t in range(NM - 1):
        te.matmul(T.pol[:, 0:P], vv(t), sl(t), start=(t == 0), stop=False)
    te.wait_ge(sem.rl3, 1)
    te.matmul(T.pol[:, 0:P], vv(3), sl(3), start=False, stop=True).then_inc(sem.m2l, 1)

    ve = g.vector
    mx = AluOpType.max
    ve.wait_ge(sem.zs, 1)
    ve.wait_ge(sem.a0, 1)
    ve.tensor_tensor(T.sr[:, 0:RC], T.px[:, 0:RC], T.zero[:, 0:RC], mx).then_inc(sem.r0, 1)
    ve.wait_ge(sem.a1, 1)
    ve.tensor_tensor(T.sr[:, RC:2 * RC], T.py[:, 0:RC], T.zero[:, 0:RC], mx).then_inc(sem.r1, 1)
    ve.wait_ge(sem.a2, 1)
    ve.tensor_tensor(T.sr[:, 2 * RC:3 * RC], T.px[:, 0:RC], T.zero[:, 0:RC], mx).then_inc(sem.r2, 1)
    ve.wait_ge(sem.a3, 1)
    ve.tensor_tensor(sa(3), T.pa[:, 0:P], T.zero[:, 0:P], mx).then_inc(sem.r3, 1)
    ve.wait_ge(sem.ab, 1)
    ve.tensor_tensor(sb(3), T.pb[:, 0:P], T.zero[:, 0:P], mx).then_inc(sem.rb, 1)
    ve.wait_ge(sem.m2a, 1)
    ve.tensor_copy(T.yo[:, 0:P], T.poa[:, 0:P]).then_inc(sem.cr, 1)
    ve.wait_ge(sem.m2b, 1)
    ve.tensor_copy(T.yo[:, P:RC], T.pob[:, 0:P]).then_inc(sem.cr, 1)
    ve.wait_ge(sem.al1, NM - 1)
    ve.tensor_tensor(T.sl[:, 0:3 * P], T.pl[:, 0:3 * P], T.zero[:, 0:3 * P], mx).then_inc(sem.rl1, 1)
    ve.wait_ge(sem.al3, 1)
    ve.tensor_tensor(sl(3), T.py[:, 0:P], T.zero[:, 0:P], mx).then_inc(sem.rl3, 1)
    ve.wait_ge(sem.m2l, 1)
    ve.tensor_copy(T.yo[:, RC:RC + P], T.pol[:, 0:P]).then_inc(sem.cl, 1)

    ymask = topo.mask(core, clients[0])
    for c in clients:
        ymask &= topo.mask(core, c)
    eng = _engines(ymask)
    share = len(eng) // CL
    g.wait_ge(sem.cr, CL)
    g.remote_dma_fused([RemoteDMATransfer(dst_ids=[_dst(topo, c, core)], dma_engine_mask=_join(eng[s * share:(s + 1) * share]),
                                          remote_sem=sem.yin, src=T.yo[:, s * P:(s + 1) * P], dst=T.yl[:, :])
                        for s, c in enumerate(clients)], local_sem=sem.sent)

    g.sync.wait_ge(sem.cl, 1)
    g.sync.dma_start(T.y[:, :], T.yo[:, RC:RC + P]).then_inc(sem.st, 16)
    g.sync.wait_ge(sem.st, 16)
    g.wait_ge(sem.sent, nkv + share * CL)


def rank_program(g, core, T, topo):
    if T.rank_of(core) is None:
        return
    sites, served = _plan(T, topo)
    if core in served:
        _site(g, core, T, topo, sites, served[core])
        return
    for s in sites:
        if core in served[s]:
            _client(g, core, T, topo, s, served[s].index(core))
